import numpy as np
import ml_dtypes


def mxq(x, axis, fmt="e4m3"):
    dtype, down = {"e4m3": (ml_dtypes.float8_e4m3fn, 7), "e5m2": (ml_dtypes.float8_e5m2, 14)}[fmt]
    v = np.moveaxis(np.asarray(x, np.float32).astype(ml_dtypes.bfloat16).astype(np.float64), axis, -1)
    blocks = v.reshape(v.shape[:-1] + (-1, 32))
    amax = np.abs(blocks).max(-1, keepdims=True)
    byte = np.maximum(np.where(amax > 0, np.frexp(amax)[1] - 1 + 127, 0) - down, 1)
    scale = np.exp2(byte - 127.0)
    codes = (blocks / scale).astype(np.float32).astype(dtype).astype(np.float64)
    return np.moveaxis((codes * scale).reshape(v.shape), -1, axis)


WIDE = False


def mx_kscale(k):
    if not WIDE:
        return np.ones(k)
    levels = np.array([10, -10, 5, -5, 0])
    if k % 512:
        return np.exp2(np.random.permutation(np.resize(levels, k // 32))).repeat(32)
    a = np.empty((k // 512, 16))
    for p in range(k // 512):
        a[p, :8] = np.random.permutation(np.resize(levels, 8))
        for g in range(8):
            far = levels[np.abs(levels - a[p, g]) >= 10]
            a[p, g + 8] = far[np.random.randint(len(far))]
    return np.exp2(a.ravel()).repeat(32)


def f64(x):
    return np.asarray(x).astype(np.float64)


def striped(idx):
    return np.tile(idx.reshape(-1, 16).T, (8, 1)).astype(np.uint16)


def unstriped(offs):
    return offs[:16].T.reshape(-1).astype(np.int64)


E2M1 = np.array([0.0, 0.5, 1.0, 1.5, 2.0, 3.0, 4.0, 6.0, -0.0, -0.5, -1.0, -1.5, -2.0, -3.0, -4.0, -6.0])


def pack_weight(w, fmt):
    k, n = w.shape
    w = f64(np.asarray(w, np.float32).astype(ml_dtypes.bfloat16)).reshape(k // 32, 32, n)
    amax = np.abs(w).max(1)
    if fmt == "e4m3":
        byte = np.frexp(amax)[1] - 1 + 127 - 7
    else:
        mant, ex = np.frexp(amax / 6.0)
        byte = np.where(mant > 0.5, ex, ex - 1) + 127
    byte = np.clip(np.where(amax > 0, byte, 1), 1, 254)
    scaled = (w * np.exp2(127.0 - byte)[:, None, :]).reshape(k, n).astype(np.float32)
    by_word = np.ascontiguousarray(scaled.reshape(k // 512, 128, 4, n).transpose(0, 1, 3, 2))
    if fmt == "e4m3":
        words = by_word.astype(ml_dtypes.float8_e4m3fn).view(np.uint8)
    else:
        c = by_word.astype(ml_dtypes.float4_e2m1fn).view(np.uint8) & 0xF
        words = (c[..., 0::2] | (c[..., 1::2] << 4)).reshape(k // 512, 128, 2 * n)
    return np.ascontiguousarray(words), np.ascontiguousarray(byte.astype(np.uint8).reshape(k // 512, 16, n))


def unpack_weight(words, scales, fmt):
    g, _, n = scales.shape
    words = np.ascontiguousarray(words).reshape(g, 128, n, -1)
    if fmt == "e4m3":
        vals = words.view(ml_dtypes.float8_e4m3fn).astype(np.float64)
    else:
        nib = np.empty((g, 128, n, 4), np.uint8)
        nib[..., 0::2] = words & 0xF
        nib[..., 1::2] = words >> 4
        vals = E2M1[nib]
    vals = vals * np.repeat(np.exp2(scales.astype(np.float64) - 127.0), 8, axis=1)[..., None]
    return vals.transpose(0, 1, 3, 2).reshape(g * 512, n)


def silu(v):
    return v / (1.0 + np.exp(-np.maximum(v, -700.0)))


K, T, E, C, H, N = 2560, 512, 2, 256, 512, 384
R = 2


def by_expert(wq, xq):
    return np.concatenate([wq[e].T @ xq[:, e * C:(e + 1) * C] for e in range(E)], axis=1)


def setup_inputs():
    n = np.random.standard_normal
    s = mx_kscale(K)[:, None]
    u = mx_kscale(H)
    slot_token = np.concatenate([r * (T // R) + np.random.permutation(T // R)[:C // R] for e in range(E) for r in range(R)])
    w1 = [pack_weight(m, "e2m1") for m in n((E, K, H)) / np.sqrt(K) / s[None]]
    w3 = [pack_weight(m, "e2m1") for m in n((E, K, H)) / np.sqrt(K) / s[None] * u[None, None, :]]
    w2 = [pack_weight(m, "e2m1") for m in n((E, H, N)) / np.sqrt(H) / u[None, :, None]]
    return {
        "xT": (n((K, T)) * s).astype(np.float32),
        "w1_words": np.stack([m[0] for m in w1]),
        "w1_scales": np.stack([m[1] for m in w1]),
        "w3_words": np.stack([m[0] for m in w3]),
        "w3_scales": np.stack([m[1] for m in w3]),
        "w2_words": np.stack([m[0] for m in w2]),
        "w2_scales": np.stack([m[1] for m in w2]),
        "offs": striped(slot_token),
    }


def reference(xT, w1_words, w1_scales, w3_words, w3_scales, w2_words, w2_scales, offs):
    idx = unstriped(offs)
    w1 = np.stack([unpack_weight(w1_words[e], w1_scales[e], "e2m1") for e in range(E)])
    w3 = np.stack([unpack_weight(w3_words[e], w3_scales[e], "e2m1") for e in range(E)])
    w2 = np.stack([unpack_weight(w2_words[e], w2_scales[e], "e2m1") for e in range(E)])
    xq = mxq(f64(xT)[:, idx], 0, "e4m3")
    h = silu(by_expert(w1, xq))
    h = h * by_expert(w3, xq)
    y = by_expert(w2, mxq(h, 0, "e4m3"))
    return y.reshape(N, E, R, C // R).transpose(0, 2, 1, 3).reshape(N, E * C)

@@ -1,0 +1,190 @@
+from contextlib import ExitStack
+
+import concourse.mybir as mybir
+from concourse.masks import make_identity
+
+K, T, E, C, H, N = 2560, 512, 2, 256, 512, 384
+R = 2
+P = 128
+PASSES = K // 512
+S = E * C
+
+FLOPS = 2 * S * (2 * K * H + H * N)
+
+F32 = mybir.dt.float32
+BF16 = mybir.dt.bfloat16
+I32 = mybir.dt.int32
+U32 = mybir.dt.uint32
+U16 = mybir.dt.uint16
+U8 = mybir.dt.uint8
+E4M3 = mybir.dt.float8_e4m3fn_x4
+E2M1 = mybir.dt.float4_e2m1fn_x4
+COPY = mybir.ActivationFunctionType.Copy
+SILU = mybir.ActivationFunctionType.Silu
+MULT = mybir.AluOpType.mult
+
+
+def tile_moe_eps_glu_silu_kernel(
+    tc, xT, w1_words, w1_scales, w3_words, w3_scales, w2_words, w2_scales, offs, out
+):
+    nc = tc.nc
+    with ExitStack() as ctx:
+        keep = ctx.enter_context(tc.tile_pool(name="keep", bufs=1))
+        psum = ctx.enter_context(tc.psum_pool(name="psum", bufs=1))
+
+        offsets = keep.tile([P, S // 16], U16, name="offsets")
+        raw = [keep.tile([P, 4, T], F32, name=f"raw{s}") for s in range(PASSES)]
+        grouped = [keep.tile([P, T, 4], BF16, name=f"grouped{s}", align_bytes=64) for s in range(PASSES)]
+        codes = keep.tile([P, (PASSES + 1) * T], I32, name="codes", align_bytes=64)
+        scales = keep.tile([P, (PASSES + 1) * T], U8, name="scales", align_bytes=64)
+        slot_codes = [keep.tile([P, S], U32, name=f"slot_codes{s}", align_bytes=64) for s in range(PASSES)]
+        slot_scales = [keep.tile([P, S], U8, name=f"slot_scales{s}", align_bytes=64) for s in range(PASSES)]
+        w1w = [keep.tile([P, E, 2 * H], U8, name=f"w1w{s}", align_bytes=64) for s in range(PASSES)]
+        w3w = [keep.tile([P, E, 2 * H], U8, name=f"w3w{s}", align_bytes=64) for s in range(PASSES)]
+        w2w = keep.tile([P, E, 2 * N], U8, name="w2w", align_bytes=64)
+        w1s = keep.tile([P, E * PASSES, H], U8, name="w1s", align_bytes=64)
+        w3s = keep.tile([P, E * PASSES, H], U8, name="w3s", align_bytes=64)
+        w2s = keep.tile([P, E, N], U8, name="w2s", align_bytes=64)
+        ident = keep.tile([P, P], F32, name="ident")
+        warm = keep.tile([P, 1], F32, name="warm")
+
+        def flat32(ap):
+            return ap.rearrange("p a b -> p (a b)").bitcast(I32)
+
+        nc.vector.memset(warm[:], 0.0)
+        nc.scalar.activation(warm[:], warm[:], SILU)
+        nc.vector.memset(flat32(w1s[:]), 0)
+        nc.vector.memset(flat32(w3s[:]), 0)
+        nc.gpsimd.memset(flat32(w2s[:]), 0)
+        nc.gpsimd.memset(codes[:, PASSES * T :], 0)
+        nc.gpsimd.memset(scales[:].bitcast(I32), 0)
+        make_identity(nc, ident[:])
+
+        def load_x(s, t0, t1):
+            src = xT[s * 512 : (s + 1) * 512, :].rearrange("(p j) t -> p j t", j=4)
+            nc.sync.dma_start(raw[s][:, :, t0:t1], src[:, :, t0:t1])
+
+        def load_w(tiles, words, s):
+            nc.sync.dma_start(
+                tiles[s][:].bitcast(I32), words[:, s].rearrange("e p b -> p e b").bitcast(I32)
+            )
+
+        def load_scales(tile, src):
+            view = src.rearrange("e s (q r) i -> r q (e s) i", r=4)
+            for r in range(4):
+                nc.sync.dma_start(tile[r:P:32].bitcast(I32), view[r].bitcast(I32))
+
+        load_x(0, 0, T // 2)
+        load_x(0, T // 2, T)
+        nc.sync.dma_start(offsets[:], offs)
+        load_x(1, 0, T)
+        load_scales(w1s, w1_scales)
+        load_scales(w3s, w3_scales)
+        load_scales(w2s, w2_scales)
+        load_w(w1w, w1_words, 0)
+        load_w(w3w, w3_words, 0)
+        for s in range(2, PASSES):
+            load_x(s, 0, T // 2)
+            load_x(s, T // 2, T)
+            load_w(w1w, w1_words, s - 1)
+            load_w(w3w, w3_words, s - 1)
+        load_w(w1w, w1_words, PASSES - 1)
+        load_w(w3w, w3_words, PASSES - 1)
+        nc.sync.dma_start(w2w[:].bitcast(I32), w2_words[:, 0].rearrange("e p b -> p e b").bitcast(I32))
+
+        def cast(s, t0, t1, on_vector):
+            dst = grouped[s][:, t0:t1, :].rearrange("p (c i) j -> p c j i", i=4)
+            src = raw[s][:, :, t0:t1].rearrange("p j (c i) -> p c j i", i=4)
+            if on_vector:
+                nc.vector.tensor_copy(dst, src)
+            else:
+                nc.scalar.activation(dst, src, COPY)
+
+        def first_column(s):
+            return (PASSES - 1 - s) * T
+
+        def quantize(s, t0, t1):
+            cols = slice(first_column(s) + t0, first_column(s) + t1)
+            nc.vector.quantize_mx(
+                out=codes[:, cols].bitcast(E4M3),
+                scales=scales[:, cols],
+                in_=grouped[s][:, t0:t1, :].rearrange("p t j -> p (t j)"),
+            )
+
+        def gather(s, e0, e1):
+            cols = slice(e0 * C, e1 * C)
+            idx = offsets[:, e0 * (C // 16) : e1 * (C // 16)]
+            width = T if e1 - e0 == 1 else 2 * T
+            window = slice(first_column(s), first_column(s) + width)
+            nc.vector.tensor_copy(slot_codes[s][:, cols], codes[:, window].bitcast(U32).indirect(idx))
+            nc.vector.tensor_copy(slot_scales[s][:, cols], scales[:, window].indirect(idx))
+
+        banks = {}
+        for e in range(E):
+            for m in range(R):
+                for g in range(2):
+                    banks[e, m, g] = psum.tile([P, H], F32, name=f"sum{e}{m}{g}", tag=f"bank{e}{m}{g}")
+
+        def multiply(s, e):
+            for g, (words, wscales) in enumerate(((w1w, w1s), (w3w, w3s))):
+                for m in range(R):
+                    cols = slice(e * C + m * P, e * C + (m + 1) * P)
+                    nc.tensor.matmul_mx(
+                        out=banks[e, m, g][:],
+                        lhsT=slot_codes[s][:, cols].bitcast(E4M3),
+                        lhsT_scale=slot_scales[s][:, cols],
+                        rhs=words[s][:, e, :].bitcast(E2M1),
+                        rhs_scale=wscales[:, e * PASSES + s, :],
+                        start=(s == 0),
+                        stop=(s == PASSES - 1),
+                    )
+
+        half = T // 2
+        for s in range(PASSES):
+            cast(s, 0, half, False)
+            cast(s, half, T, s == 0)
+            quantize(s, 0, T)
+            if s < PASSES - 1:
+                gather(s, 0, E)
+                for e in range(E):
+                    multiply(s, e)
+            else:
+                for e in range(E):
+                    gather(s, e, e + 1)
+                    multiply(s, e)
+
+        units = [(e, m) for e in range(E) for m in range(R)]
+        for e, m in units:
+            gate = keep.tile([P, H], F32, name=f"gate{e}{m}")
+            nc.scalar.activation(gate[:], banks[e, m, 0][:], SILU)
+            hidden = keep.tile([P, H], BF16, name=f"hidden{e}{m}", align_bytes=64)
+            nc.vector.tensor_tensor(hidden[:], banks[e, m, 1][:], gate[:], MULT)
+            turned = psum.tile([P, 2, P], F32, name=f"turned{e}{m}", tag=f"bank{e}{m}0")
+            words = hidden[:].bitcast(F32)
+            for u in range(2):
+                nc.tensor.transpose(turned[:, u, :], words[:, u : H // 2 : 2], ident[:])
+            hg = keep.tile([P, P, 4], BF16, name=f"hg{e}{m}", align_bytes=64)
+            hg_flat = hg[:].rearrange("p r j -> p (r j)")
+            nc.scalar.copy(
+                hg_flat.bitcast(F32).rearrange("p (r u) -> p r u", u=2), turned[:].rearrange("p u r -> p r u")
+            )
+            h_codes = keep.tile([P, P], U32, name=f"h_codes{e}{m}", align_bytes=64)
+            h_scales = keep.tile([P, P], U8, name=f"h_scales{e}{m}", align_bytes=64)
+            nc.vector.quantize_mx(out=h_codes[:].bitcast(E4M3), scales=h_scales[:], in_=hg_flat)
+            y = psum.tile([P, N // P, P], F32, name=f"y{e}{m}", tag=f"bank{e}{m}1")
+            for j in range(N // P):
+                nc.tensor.matmul_mx(
+                    out=y[:, j, :],
+                    lhsT=w2w[:, e, 2 * P * j : 2 * P * (j + 1)].bitcast(E2M1),
+                    lhsT_scale=w2s[:, e, P * j : P * (j + 1)],
+                    rhs=h_codes[:].bitcast(E4M3),
+                    rhs_scale=h_scales[:],
+                    start=True,
+                    stop=True,
+                )
+            result = keep.tile([P, N // P, P], F32, name=f"result{e}{m}")
+            nc.scalar.activation(result[:], y[:], COPY)
+            col = C * m + P * e
+            nc.sync.dma_start(
+                out[:, col : col + P].rearrange("(j p) u -> p j u", p=P), result[:]
+            )

@@ -60,9 +60,10 @@ def tile_moe_eps_glu_silu_kernel(
         nc.gpsimd.memset(scales[:].bitcast(I32), 0)
         make_identity(nc, ident[:])
 
-        def load_x(s, t0, t1):
-            src = xT[s * 512 : (s + 1) * 512, :].rearrange("(p j) t -> p j t", j=4)
-            nc.sync.dma_start(raw[s][:, :, t0:t1], src[:, :, t0:t1])
+        half = T // 2
+
+        def load_x(s):
+            nc.sync.dma_start(raw[s][:], xT[s * 512 : (s + 1) * 512, :].rearrange("(p j) t -> p j t", j=4))
 
         def load_w(tiles, words, s):
             nc.sync.dma_start(
@@ -74,23 +75,19 @@ def tile_moe_eps_glu_silu_kernel(
             for r in range(4):
                 nc.sync.dma_start(tile[r:P:32].bitcast(I32), view[r].bitcast(I32))
 
-        load_x(0, 0, T // 2)
-        load_x(0, T // 2, T)
+        load_x(0)
         nc.sync.dma_start(offsets[:], offs)
-        load_x(1, 0, T)
+        load_x(1)
+        load_x(2)
         load_scales(w1s, w1_scales)
         load_scales(w3s, w3_scales)
-        load_scales(w2s, w2_scales)
-        load_w(w1w, w1_words, 0)
-        load_w(w3w, w3_words, 0)
-        for s in range(2, PASSES):
-            load_x(s, 0, T // 2)
-            load_x(s, T // 2, T)
-            load_w(w1w, w1_words, s - 1)
-            load_w(w3w, w3_words, s - 1)
-        load_w(w1w, w1_words, PASSES - 1)
-        load_w(w3w, w3_words, PASSES - 1)
+        for s in range(PASSES):
+            load_w(w1w, w1_words, s)
+            load_w(w3w, w3_words, s)
+            if s + 3 < PASSES:
+                load_x(s + 3)
         nc.sync.dma_start(w2w[:].bitcast(I32), w2_words[:, 0].rearrange("e p b -> p e b").bitcast(I32))
+        load_scales(w2s, w2_scales)
 
         def cast(s, t0, t1, on_vector):
             dst = grouped[s][:, t0:t1, :].rearrange("p (c i) j -> p c j i", i=4)
@@ -139,22 +136,18 @@ def tile_moe_eps_glu_silu_kernel(
                         stop=(s == PASSES - 1),
                     )
 
-        half = T // 2
         for s in range(PASSES):
             cast(s, 0, half, False)
             cast(s, half, T, s == 0)
             quantize(s, 0, T)
-            if s < PASSES - 1:
+            if s < PASSES - 2:
                 gather(s, 0, E)
                 for e in range(E):
                     multiply(s, e)
             else:
-                for e in range(E):
-                    gather(s, e, e + 1)
-                    multiply(s, e)
-
-        units = [(e, m) for e in range(E) for m in range(R)]
-        for e, m in units:
+                gather(s, 0, 1)
+                multiply(s, 0)
+        def finish(e, m):
             gate = keep.tile([P, H], F32, name=f"gate{e}{m}")
             nc.scalar.activation(gate[:], banks[e, m, 0][:], SILU)
             hidden = keep.tile([P, H], BF16, name=f"hidden{e}{m}", align_bytes=64)
@@ -183,8 +176,19 @@ def tile_moe_eps_glu_silu_kernel(
                     stop=True,
                 )
             result = keep.tile([P, N // P, P], F32, name=f"result{e}{m}")
-            nc.scalar.activation(result[:], y[:], COPY)
+            if m == 0:
+                nc.scalar.copy(result[:], y[:])
+            else:
+                nc.vector.tensor_copy(result[:], y[:])
             col = C * m + P * e
             nc.sync.dma_start(
                 out[:, col : col + P].rearrange("(j p) u -> p j u", p=P), result[:]
             )
+
+        for m in range(R):
+            finish(0, m)
+        for s in range(PASSES - 2, PASSES):
+            gather(s, 1, 2)
+            multiply(s, 1)
+        for m in range(R):
+            finish(1, m)

@@ -78,14 +78,15 @@ def tile_moe_eps_glu_silu_kernel(
         load_x(0)
         nc.sync.dma_start(offsets[:], offs)
         load_x(1)
-        load_x(2)
         load_scales(w1s, w1_scales)
+        load_x(2)
         load_scales(w3s, w3_scales)
+        load_x(3)
         for s in range(PASSES):
             load_w(w1w, w1_words, s)
             load_w(w3w, w3_words, s)
-            if s + 3 < PASSES:
-                load_x(s + 3)
+            if s == 1:
+                load_x(4)
         nc.sync.dma_start(w2w[:].bitcast(I32), w2_words[:, 0].rearrange("e p b -> p e b").bitcast(I32))
         load_scales(w2s, w2_scales)
 
@@ -139,7 +140,11 @@ def tile_moe_eps_glu_silu_kernel(
         for s in range(PASSES):
             cast(s, 0, half, False)
             cast(s, half, T, s == 0)
-            quantize(s, 0, T)
+            if s < PASSES - 1:
+                quantize(s, 0, T)
+            else:
+                quantize(s, 0, half)
+                quantize(s, half, T)
             if s < PASSES - 2:
                 gather(s, 0, E)
                 for e in range(E):
@@ -158,9 +163,8 @@ def tile_moe_eps_glu_silu_kernel(
                 nc.tensor.transpose(turned[:, u, :], words[:, u : H // 2 : 2], ident[:])
             hg = keep.tile([P, P, 4], BF16, name=f"hg{e}{m}", align_bytes=64)
             hg_flat = hg[:].rearrange("p r j -> p (r j)")
-            nc.scalar.copy(
-                hg_flat.bitcast(F32).rearrange("p (r u) -> p r u", u=2), turned[:].rearrange("p u r -> p r u")
-            )
+            copy_turned = nc.vector.tensor_copy if (e, m) == (1, 1) else nc.scalar.copy
+            copy_turned(hg_flat.bitcast(F32).rearrange("p (r u) -> p r u", u=2), turned[:].rearrange("p u r -> p r u"))
             h_codes = keep.tile([P, P], U32, name=f"h_codes{e}{m}", align_bytes=64)
             h_scales = keep.tile([P, P], U8, name=f"h_scales{e}{m}", align_bytes=64)
             nc.vector.quantize_mx(out=h_codes[:].bitcast(E4M3), scales=h_scales[:], in_=hg_flat)
@@ -185,10 +189,9 @@ def tile_moe_eps_glu_silu_kernel(
                 out[:, col : col + P].rearrange("(j p) u -> p j u", p=P), result[:]
             )
 
-        for m in range(R):
-            finish(0, m)
         for s in range(PASSES - 2, PASSES):
             gather(s, 1, 2)
             multiply(s, 1)
-        for m in range(R):
-            finish(1, m)
+        for e in range(E):
+            for m in range(R):
+                finish(e, m)

from contextlib import ExitStack

import concourse.mybir as mybir
from concourse.masks import make_identity

K, T, E, C, H, N = 2560, 512, 2, 256, 512, 384
R = 2
P = 128
PASSES = K // 512
S = E * C

FLOPS = 2 * S * (2 * K * H + H * N)

F32 = mybir.dt.float32
BF16 = mybir.dt.bfloat16
I32 = mybir.dt.int32
U32 = mybir.dt.uint32
U16 = mybir.dt.uint16
U8 = mybir.dt.uint8
E4M3 = mybir.dt.float8_e4m3fn_x4
E2M1 = mybir.dt.float4_e2m1fn_x4
COPY = mybir.ActivationFunctionType.Copy
SILU = mybir.ActivationFunctionType.Silu
MULT = mybir.AluOpType.mult


def tile_moe_eps_glu_silu_kernel(
    tc, xT, w1_words, w1_scales, w3_words, w3_scales, w2_words, w2_scales, offs, out
):
    nc = tc.nc
    with ExitStack() as ctx:
        keep = ctx.enter_context(tc.tile_pool(name="keep", bufs=1))
        psum = ctx.enter_context(tc.psum_pool(name="psum", bufs=1))

        offsets = keep.tile([P, S // 16], U16, name="offsets")
        raw = [keep.tile([P, 4, T], F32, name=f"raw{s}") for s in range(PASSES)]
        grouped = [keep.tile([P, T, 4], BF16, name=f"grouped{s}", align_bytes=64) for s in range(PASSES)]
        codes = keep.tile([P, (PASSES + 1) * T], I32, name="codes", align_bytes=64)
        scales = keep.tile([P, (PASSES + 1) * T], U8, name="scales", align_bytes=64)
        slot_codes = [keep.tile([P, S], U32, name=f"slot_codes{s}", align_bytes=64) for s in range(PASSES)]
        slot_scales = [keep.tile([P, S], U8, name=f"slot_scales{s}", align_bytes=64) for s in range(PASSES)]
        w1w = [keep.tile([P, E, 2 * H], U8, name=f"w1w{s}", align_bytes=64) for s in range(PASSES)]
        w3w = [keep.tile([P, E, 2 * H], U8, name=f"w3w{s}", align_bytes=64) for s in range(PASSES)]
        w2w = keep.tile([P, E, 2 * N], U8, name="w2w", align_bytes=64)
        w1s = keep.tile([P, E * PASSES, H], U8, name="w1s", align_bytes=64)
        w3s = keep.tile([P, E * PASSES, H], U8, name="w3s", align_bytes=64)
        w2s = keep.tile([P, E, N], U8, name="w2s", align_bytes=64)
        ident = keep.tile([P, P], F32, name="ident")
        warm = keep.tile([P, 1], F32, name="warm")

        def flat32(ap):
            return ap.rearrange("p a b -> p (a b)").bitcast(I32)

        nc.vector.memset(warm[:], 0.0)
        nc.scalar.activation(warm[:], warm[:], SILU)
        nc.vector.memset(flat32(w1s[:]), 0)
        nc.vector.memset(flat32(w3s[:]), 0)
        nc.gpsimd.memset(flat32(w2s[:]), 0)
        nc.gpsimd.memset(codes[:, PASSES * T :], 0)
        nc.gpsimd.memset(scales[:].bitcast(I32), 0)
        make_identity(nc, ident[:])

        half = T // 2

        def load_x(s):
            nc.sync.dma_start(raw[s][:], xT[s * 512 : (s + 1) * 512, :].rearrange("(p j) t -> p j t", j=4))

        def load_w(tiles, words, s):
            nc.sync.dma_start(
                tiles[s][:].bitcast(I32), words[:, s].rearrange("e p b -> p e b").bitcast(I32)
            )

        def load_scales(tile, src):
            view = src.rearrange("e s (q r) i -> r q (e s) i", r=4)
            for r in range(4):
                nc.sync.dma_start(tile[r:P:32].bitcast(I32), view[r].bitcast(I32))

        load_x(0)
        nc.sync.dma_start(offsets[:], offs)
        load_x(1)
        load_scales(w1s, w1_scales)
        load_x(2)
        load_scales(w3s, w3_scales)
        load_x(3)
        for s in range(PASSES):
            load_w(w1w, w1_words, s)
            load_w(w3w, w3_words, s)
            if s == 1:
                load_x(4)
        nc.sync.dma_start(w2w[:].bitcast(I32), w2_words[:, 0].rearrange("e p b -> p e b").bitcast(I32))
        load_scales(w2s, w2_scales)

        def cast(s, t0, t1, on_vector):
            dst = grouped[s][:, t0:t1, :].rearrange("p (c i) j -> p c j i", i=4)
            src = raw[s][:, :, t0:t1].rearrange("p j (c i) -> p c j i", i=4)
            if on_vector:
                nc.vector.tensor_copy(dst, src)
            else:
                nc.scalar.activation(dst, src, COPY)

        def first_column(s):
            return (PASSES - 1 - s) * T

        def quantize(s, t0, t1):
            cols = slice(first_column(s) + t0, first_column(s) + t1)
            nc.vector.quantize_mx(
                out=codes[:, cols].bitcast(E4M3),
                scales=scales[:, cols],
                in_=grouped[s][:, t0:t1, :].rearrange("p t j -> p (t j)"),
            )

        def gather(s, e0, e1):
            cols = slice(e0 * C, e1 * C)
            idx = offsets[:, e0 * (C // 16) : e1 * (C // 16)]
            width = T if e1 - e0 == 1 else 2 * T
            window = slice(first_column(s), first_column(s) + width)
            nc.vector.tensor_copy(slot_codes[s][:, cols], codes[:, window].bitcast(U32).indirect(idx))
            nc.vector.tensor_copy(slot_scales[s][:, cols], scales[:, window].indirect(idx))

        banks = {}
        for e in range(E):
            for m in range(R):
                for g in range(2):
                    banks[e, m, g] = psum.tile([P, H], F32, name=f"sum{e}{m}{g}", tag=f"bank{e}{m}{g}")

        def multiply(s, e):
            for g, (words, wscales) in enumerate(((w1w, w1s), (w3w, w3s))):
                for m in range(R):
                    cols = slice(e * C + m * P, e * C + (m + 1) * P)
                    nc.tensor.matmul_mx(
                        out=banks[e, m, g][:],
                        lhsT=slot_codes[s][:, cols].bitcast(E4M3),
                        lhsT_scale=slot_scales[s][:, cols],
                        rhs=words[s][:, e, :].bitcast(E2M1),
                        rhs_scale=wscales[:, e * PASSES + s, :],
                        start=(s == 0),
                        stop=(s == PASSES - 1),
                    )

        for s in range(PASSES):
            cast(s, 0, half, False)
            cast(s, half, T, s == 0)
            if s < PASSES - 1:
                quantize(s, 0, T)
            else:
                quantize(s, 0, half)
                quantize(s, half, T)
            if s < PASSES - 2:
                gather(s, 0, E)
                for e in range(E):
                    multiply(s, e)
            else:
                gather(s, 0, 1)
                multiply(s, 0)
        def finish(e, m):
            gate = keep.tile([P, H], F32, name=f"gate{e}{m}")
            nc.scalar.activation(gate[:], banks[e, m, 0][:], SILU)
            hidden = keep.tile([P, H], BF16, name=f"hidden{e}{m}", align_bytes=64)
            nc.vector.tensor_tensor(hidden[:], banks[e, m, 1][:], gate[:], MULT)
            turned = psum.tile([P, 2, P], F32, name=f"turned{e}{m}", tag=f"bank{e}{m}0")
            words = hidden[:].bitcast(F32)
            for u in range(2):
                nc.tensor.transpose(turned[:, u, :], words[:, u : H // 2 : 2], ident[:])
            hg = keep.tile([P, P, 4], BF16, name=f"hg{e}{m}", align_bytes=64)
            hg_flat = hg[:].rearrange("p r j -> p (r j)")
            copy_turned = nc.vector.tensor_copy if (e, m) == (1, 1) else nc.scalar.copy
            copy_turned(hg_flat.bitcast(F32).rearrange("p (r u) -> p r u", u=2), turned[:].rearrange("p u r -> p r u"))
            h_codes = keep.tile([P, P], U32, name=f"h_codes{e}{m}", align_bytes=64)
            h_scales = keep.tile([P, P], U8, name=f"h_scales{e}{m}", align_bytes=64)
            nc.vector.quantize_mx(out=h_codes[:].bitcast(E4M3), scales=h_scales[:], in_=hg_flat)
            y = psum.tile([P, N // P, P], F32, name=f"y{e}{m}", tag=f"bank{e}{m}1")
            for j in range(N // P):
                nc.tensor.matmul_mx(
                    out=y[:, j, :],
                    lhsT=w2w[:, e, 2 * P * j : 2 * P * (j + 1)].bitcast(E2M1),
                    lhsT_scale=w2s[:, e, P * j : P * (j + 1)],
                    rhs=h_codes[:].bitcast(E4M3),
                    rhs_scale=h_scales[:],
                    start=True,
                    stop=True,
                )
            result = keep.tile([P, N // P, P], F32, name=f"result{e}{m}")
            if m == 0:
                nc.scalar.copy(result[:], y[:])
            else:
                nc.vector.tensor_copy(result[:], y[:])
            col = C * m + P * e
            nc.sync.dma_start(
                out[:, col : col + P].rearrange("(j p) u -> p j u", p=P), result[:]
            )

        for s in range(PASSES - 2, PASSES):
            gather(s, 1, 2)
            multiply(s, 1)
        for e in range(E):
            for m in range(R):
                finish(e, m)
